import numpy as np
CORES = [33,34,161,162,289,290,417,418]
N = 8
R, B, K = 4096, 256, 2
T = B * K
CAPP = 128
def entries(a): return a.T.reshape(-1)
def pack(v, P): return np.ascontiguousarray(np.asarray(v, np.int32).reshape(-1, P).T)
def lists(rng, how):
    I = rng.integers(0, N * R, (N, T))
    O = np.stack([rng.permutation(np.repeat(np.arange(N), CAPP))[:T] for r in range(N)])
    if how == "full": O = np.stack([rng.permutation(np.repeat(rng.permutation(N)[:T // CAPP], CAPP)) for r in range(N)])
    I = R * O + rng.integers(0, R, (N, T))
    if how == "alike": I = R * O + rng.integers(0, R, (N, 1))
    if how == "edge": I = R * O + np.where(rng.random((N, T)) < 0.5, 0, R - 1)
    if how == "sorted": I = np.sort(I, axis=1)
    return {"idx": np.stack([pack(I[r], 16) for r in range(N)])}
def setup_inputs(rng):
    return dict({"tab": rng.standard_normal((N, 128, R), dtype=np.float32)}, **lists(rng, "uniform"))
def setup_inputs_alike(rng):
    d = setup_inputs(rng); d.update(lists(rng, "alike"))
    for k in ("tab",): d[k] = (d[k].astype(np.float32) * 1024.0).astype(d[k].dtype)
    return d
def setup_inputs_edge(rng):
    d = setup_inputs(rng); d.update(lists(rng, "edge"))
    for k in ("tab",): d[k] = (d[k].astype(np.float32) * (1 / 1024.0)).astype(d[k].dtype)
    return d
def setup_inputs_full(rng):
    d = setup_inputs(rng); d.update(lists(rng, "full"))
    return d
def setup_inputs_sorted(rng):
    d = setup_inputs(rng); d.update(lists(rng, "sorted"))
    return d
def check_inputs(x):
    bad = []
    if x["idx"].min() < 0 or x["idx"].max() >= N * R: bad.append("idx out of range")
    if max(int(np.bincount(entries(a) // R, minlength=N).max()) for a in x["idx"]) > CAPP: bad.append("more than CAPP entries of a list point into one rank's part")
    return bad
def reference(tab, idx):
    A = np.concatenate(list(tab), axis=1).astype(np.float64)
    return {"y": np.stack([A[:, entries(idx[r])].reshape(128, B, K).sum(axis=2) for r in range(N)]).astype(np.float32)}

@@ -1,0 +1,319 @@
+from concourse.bass import DstId, RemoteDMATransfer
+from concourse.mybir import AluOpType, ActivationFunctionType
+
+Op, Act = AluOpType, ActivationFunctionType
+NR, COLS, CAP, BAGS = 8, 4096, 128, 256
+CA = 2560
+
+SCRATCH = {
+    "tabs": ("sbuf", [128, COLS], "float32"),
+    "ei": ("sbuf", [128, 4], "int32"),
+    "owni": ("sbuf", [128, 4], "int32"),
+    "loci": ("sbuf", [128, 4], "int32"),
+    "locf": ("sbuf", [128, 4], "float32"),
+    "pidx": ("sbuf", [128, 1], "int32"),
+    "pbit": ("sbuf", [128, 1], "int32"),
+    "ptmp": ("sbuf", [128, 2], "int32"),
+    "pcol": ("sbuf", [128, 2], "float32"),
+    "offa": ("sbuf", [128, 2], "uint16"),
+    "iotar": ("sbuf", [128, 32], "int32"),
+    "rst": ("sbuf", [128, 32], "float32"),
+    "ohp": ("sbuf", [128, 56], "bfloat16"),
+    "ones": ("sbuf", [128, 128], "bfloat16"),
+    "tri": ("sbuf", [128, 128], "bfloat16"),
+    "crow": ("sbuf", [128, 32], "bfloat16"),
+    "prod": ("sbuf", [128, 32], "float32"),
+    "seg": ("sbuf", [128, 32], "float32"),
+    "ti": ("sbuf", [128, 4], "int32"),
+    "hi": ("sbuf", [128, 4], "int32"),
+    "hf": ("sbuf", [128, 4], "float32"),
+    "im16": ("sbuf", [128, 128], "float32"),
+    "i64": ("sbuf", [128, 64], "float32"),
+    "lh": ("sbuf", [128, 512], "float32"),
+    "rh": ("sbuf", [128, 256], "float32"),
+    "rq": ("sbuf", [128, 64], "uint16"),
+    "reqland": ("sbuf", [128, 512], "uint16"),
+    "stage": ("sbuf", [128, 7 * CAP], "float32"),
+    "land": ("sbuf", [128, NR * CAP], "float32"),
+    "xw": ("sbuf", [128, 144], "float32"),
+    "mw": ("sbuf", [128, 144], "float32"),
+    "m16": ("sbuf", [128, 16], "float32"),
+    "rfin": ("sbuf", [128, 64], "float32"),
+    "fu": ("sbuf", [128, 32], "uint16"),
+    "tmpo": ("sbuf", [128, BAGS], "float32"),
+    "ysb": ("sbuf", [128, BAGS], "float32"),
+    "xq": ("sbuf", [128, 64], "uint16"),
+    "xd": ("sbuf", [128, 2 * CAP], "float32"),
+    "cnt": ("psum", [128, 512], "float32"),
+    "rqp": ("psum", [128, 512], "float32"),
+    "fp": ("psum", [128, 512], "float32"),
+}
+SEMAPHORES = ["ld", "ta", "tb", "v", "p", "a", "gq", "s1", "snt", "arr", "xd0", "xd1", "st"] + ["rq%d" % q for q in range(NR)]
+
+_CACHE = {}
+
+
+def _plan(T, topo):
+    if "plan" in _CACHE:
+        return _CACHE["plan"]
+    ranks = list(T.cores)
+    world = range(4 * topo.CORES_PER_HOST)
+
+    def on_chip(c):
+        return [x for x in world if topo.host(x) == topo.host(c) and topo.chip(x) == topo.chip(c)]
+
+    peer, S, X, D, helper, relay, role, pos = {}, {}, {}, {}, {}, {}, {}, {}
+    for s in ranks:
+        mine = [x for x in ranks if x in on_chip(s)]
+        pos[s] = mine.index(s)
+        peer[s] = [x for x in mine if x != s][0]
+        S[s] = [x for x in ranks if topo.same_plane(s, x)]
+        D[s] = [x for x in ranks if not topo.may_write(s, x)]
+        X[s] = [x for x in ranks if x not in mine and x not in S[s] and x not in D[s]]
+        role[s] = ("rank",)
+    for s in ranks:
+        free = [x for x in on_chip(s) if x not in ranks and topo.die(x) == topo.die(s)]
+        helper[s] = free[pos[s]]
+        role[helper[s]] = ("helper", s)
+        far = [x for x in on_chip(X[s][0]) if x not in ranks and topo.die(x) != topo.die(X[s][0])]
+        for d in D[s]:
+            r = far[2 * pos[s] + pos[d]]
+            relay[(s, d)] = r
+            role[r] = ("relay", s, d)
+    _CACHE["plan"] = dict(peer=peer, S=S, X=X, D=D, helper=helper, relay=relay, role=role)
+    return _CACHE["plan"]
+
+
+def _bits(m):
+    return [1 << i for i in range(m.bit_length()) if (m >> i) & 1]
+
+
+def _n(m):
+    return len(_bits(m))
+
+
+def _passer(g, core, T, topo, s, outs):
+    qs = T.rank_of(s)
+    m = topo.mask(core, outs[0])
+    rsem = T.sem["rq%d" % qs]
+    nin = _n(topo.mask(s, core) & ~topo.mask(s, outs[0]))
+    g.wait_ge(rsem, nin)
+    ids = []
+    for d in outs:
+        rid, pid = topo.addr(d, core)
+        ids.append(DstId(rid=rid, pnc=pid))
+    if len(outs) == 1:
+        o = T.rank_of(outs[0])
+        src, dst = T.xq[:, 8 * o:8 * o + 8], T.reqland[:, 64 * qs + 8 * o:64 * qs + 8 * o + 8]
+    else:
+        src, dst = T.xq[:, :], T.reqland[:, 64 * qs:64 * qs + 64]
+    g.remote_dma_fused([RemoteDMATransfer(dst_ids=ids, dma_engine_mask=m, remote_sem=rsem, srcs=[src],
+                                          dsts=[dst for d in outs], alu_op=0)], local_sem=T.sem.snt)
+    for i, d in enumerate(outs):
+        rid, pid = topo.addr(d, core)
+        g.wait_ge(T.sem["xd%d" % i], nin)
+        g.remote_dma(out_ap=T.land[:, CAP * qs:CAP * qs + CAP], in_ap=T.xd[:, CAP * i:CAP * i + CAP], remote_sem=T.sem.arr,
+                     local_sem=T.sem.snt, pid=pid, routing_id=rid, dma_engine_mask=m)
+    g.wait_ge(T.sem.snt, _n(m) * (1 + len(outs)))
+
+
+def rank_program(g, core, T, topo):
+    plan = _plan(T, topo)
+    role = plan["role"].get(core)
+    if role is None:
+        return
+    if role[0] == "helper":
+        _passer(g, core, T, topo, role[1], plan["S"][role[1]])
+        return
+    if role[0] == "relay":
+        _passer(g, core, T, topo, role[1], [role[2]])
+        return
+
+    me = T.rank_of(core)
+    peer, S, X, D = plan["peer"][core], plan["S"][core], plan["X"][core], plan["D"][core]
+    helper = plan["helper"][core]
+    relays = [plan["relay"][(core, d)] for d in D]
+    lo = topo.mask(core, X[0])
+    hi = topo.mask(core, peer) & ~lo
+    lob = _bits(lo)
+    lo_a, lo_b = sum(lob[:len(lob) // 2]), sum(lob[len(lob) // 2:])
+
+    def did(d):
+        rid, pid = topo.addr(d, core)
+        return DstId(rid=rid, pnc=pid)
+
+    Q = {"v": g.vector, "p": g.tensor, "a": g.scalar, "gq": g, "s": g.sync}
+    cnt = {"v": 0, "p": 0, "a": 0, "gq": 0}
+    seen = {}
+
+    def need(q, sem, val):
+        if val > seen.get((q, sem), 0):
+            Q[q].wait_ge(T.sem[sem], val)
+            seen[(q, sem)] = val
+
+    def pre(q):
+        need(q, q, cnt[q])
+
+    def done(q, ins):
+        ins.then_inc(T.sem[q], 1)
+        cnt[q] += 1
+        return cnt[q]
+
+    V, PE, A = g.vector, g.tensor, g.scalar
+
+    def v_(fn, *a, **k):
+        pre("v")
+        return done("v", fn(*a, **k))
+
+    def g_(fn, *a, **k):
+        pre("gq")
+        return done("gq", fn(*a, **k))
+
+    def a_(*a, **k):
+        pre("a")
+        return done("a", A.activation(*a, **k))
+
+    g.sync.dma_start(T.ei[:, :], T.idx[:, :]).then_inc(T.sem.ld, 16)
+    g.sync.dma_start(T.tabs[:, 0:CA], T.tab[:, 0:CA]).then_inc(T.sem.ta, 16)
+    A.wait_ge(T.sem.s1, _n(lo) + _n(hi))
+    A.dma_start(T.tabs[:, CA:COLS], T.tab[:, CA:COLS]).then_inc(T.sem.tb, 16)
+
+    v_ones = v_(V.memset, T.ones[:, :], 1.0)
+    v_(V.memset, T.ohp[:, 0:24], 0.0)
+    g_pidx = g_(g.iota, T.pidx[:, :], [[0, 1]], 0, 1)
+    g_iotar = g_(g.iota, T.iotar[:, :], [[0, 4], [1, 8]], 0, 0)
+    g_crow = g_(g.iota, T.crow[0:1, :], [[0, 4], [CAP, 8]], 0, 0, allow_small_or_imprecise_dtypes=True)
+    need("gq", "v", v_ones)
+    g_tri = g_(g.affine_select, T.tri[:, :], T.ones[:, :], [[1, 128]], Op.is_gt, 0.0, 0, -1)
+    g_im16 = g_(g.iota, T.im16[:, :], [[0, 8], [1, 16]], 0, 0, allow_small_or_imprecise_dtypes=True)
+    g_i64 = g_(g.iota, T.i64[:, :], [[16, 64]], 0, 0, allow_small_or_imprecise_dtypes=True)
+    g_xw = g_(g.iota, T.xw[:, :], [[0, 9], [-100, 2], [1, 8]], 100, 0, allow_small_or_imprecise_dtypes=True)
+
+    need("v", "gq", g_pidx)
+    v_(V.tensor_scalar, T.pbit[:, :], T.pidx[:, :], 3, 1, Op.logical_shift_right, Op.bitwise_and)
+    v_(V.tensor_scalar, T.offa[:, 0:1], T.pbit[:, :], 0, None, Op.add)
+    v_(V.tensor_scalar, T.offa[:, 1:2], T.pbit[:, :], 2, None, Op.add)
+    need("v", "gq", g_iotar)
+    v_(V.tensor_scalar, T.rst[:, :], T.iotar[:, :], 0, None, Op.not_equal)
+
+    need("p", "gq", g_crow)
+    need("p", "v", v_ones)
+    PE.matmul(T.cnt[:, 0:32], T.ones[0:1, :], T.crow[0:1, :], True, False)
+
+    need("v", "ld", 16)
+    v_(V.tensor_scalar, T.owni[:, :], T.ei[:, :], 12, None, Op.logical_shift_right)
+    v_oh = v_(V.tensor_tensor, T.ohp[:, 24:56], T.owni[:, 0:4].indirect(T.offa[:, 0:2]), T.iotar[:, :], Op.is_equal)
+    need("p", "v", v_oh)
+    need("p", "gq", g_tri)
+    PE.matmul(T.cnt[:, 0:32], T.tri[:, :], T.ohp[:, 24:56], False, False)
+    for k in (1, 2, 3):
+        ins = PE.matmul(T.cnt[:, 0:32], T.ones[:, :], T.ohp[:, 24 - 8 * k:56 - 8 * k], False, k == 3)
+    p_cnt = done("p", ins)
+    v_(V.tensor_scalar, T.loci[:, :], T.ei[:, :], COLS - 1, None, Op.bitwise_and)
+    v_(V.tensor_copy, T.locf[:, :], T.loci[:, :])
+    need("v", "p", p_cnt)
+    v_(V.tensor_tensor, T.prod[:, :], T.ohp[:, 24:56], T.cnt[:, 0:32], Op.mult)
+    v_(V.tensor_tensor_scan, T.seg[:, :], T.rst[:, :], T.prod[:, :], 0.0, Op.mult, Op.add)
+    v_(V.tensor_copy, T.ti[:, :], T.seg[:, 7:32:8])
+    v_(V.tensor_scalar, T.hi[:, :], T.ti[:, :], NR * CAP - 16, None, Op.bitwise_and)
+    v_(V.tensor_copy, T.hf[:, :], T.hi[:, :])
+
+    need("v", "gq", g_i64)
+    for C in range(4):
+        t_c, h_c = T.seg[:, 8 * C + 7:8 * C + 8], T.hf[:, C:C + 1]
+        v_(V.tensor_scalar, T.rh[:, 64 * C:64 * C + 64], T.i64[:, :], h_c, T.locf[:, C:C + 1], Op.is_equal, Op.mult)
+        k = v_(V.tensor_scalar, T.lh[:, 128 * C:128 * C + 128], T.im16[:, :], h_c, t_c, Op.add, Op.is_equal)
+        need("p", "v", k)
+        ins = PE.matmul(T.rqp[:, 0:64], T.lh[:, 128 * C:128 * C + 128], T.rh[:, 64 * C:64 * C + 64], C == 0, C == 3)
+    p_rq = done("p", ins)
+    need("v", "p", p_rq)
+    v_rq = v_(V.tensor_copy, T.rq[:, :], T.rqp[:, 0:64])
+
+    mysem = T.sem["rq%d" % me]
+    slot = T.reqland[:, 64 * me:64 * me + 64]
+    need("gq", "v", v_rq)
+    g.remote_dma_fused([
+        RemoteDMATransfer(dst_ids=[did(r) for r in relays], dma_engine_mask=lo, remote_sem=mysem, srcs=[T.rq[:, :]],
+                          dsts=[T.xq[:, :] for r in relays], alu_op=0),
+        RemoteDMATransfer(dst_ids=[did(helper), did(peer)], dma_engine_mask=hi, remote_sem=mysem, srcs=[T.rq[:, :]],
+                          dsts=[T.xq[:, :], slot], alu_op=0),
+    ], local_sem=T.sem.s1)
+    g.remote_dma_fused([
+        RemoteDMATransfer(dst_ids=[did(d) for d in X], dma_engine_mask=lo, remote_sem=mysem, srcs=[T.rq[:, :]],
+                          dsts=[slot for d in X], alu_op=0),
+    ], local_sem=T.sem.snt)
+    sent = _n(lo)
+
+    v_(V.tensor_scalar, T.ptmp[:, 0:1], T.pidx[:, :], 15, None, Op.bitwise_and)
+    v_(V.tensor_scalar, T.ptmp[:, 1:2], T.pidx[:, :], 4, None, Op.logical_shift_right)
+    v_(V.tensor_copy, T.pcol[:, :], T.ptmp[:, :])
+    v_(V.tensor_scalar, T.m16[:, :], T.im16[:, 0:16], T.pcol[:, 0:1], None, Op.is_equal)
+    need("v", "gq", g_xw)
+    v_(V.tensor_scalar, T.mw[:, :], T.xw[:, :], T.pcol[:, 1:2], None, Op.is_equal)
+    for eta in (0, 1):
+        for nu in (0, 1):
+            C = 2 * nu + eta
+            k = v_(V.tensor_scalar, T.rfin[:, 32 * eta + nu:32 * eta + 32:2], T.m16[:, :], T.seg[:, 8 * C + 7:8 * C + 8], None,
+                   Op.mult)
+    need("p", "v", k)
+    PE.matmul(T.fp[:, 0:32], T.mw[:, 8:136], T.rfin[:, 0:32], True, False)
+    p_f = done("p", PE.matmul(T.fp[:, 0:32], T.mw[:, 0:128], T.rfin[:, 32:64], False, True))
+    need("v", "p", p_f)
+    v_fu = v_(V.tensor_copy, T.fu[:, :], T.fp[:, 0:32])
+
+    order = [D[0], S[0], D[1], S[1], X[0], X[1], peer]
+    win = T.tabs[:, 0:COLS]
+    ready = []
+    for q in ("v", "a"):
+        need(q, "ta", 16)
+        need(q, "tb", 16)
+    for k, d in enumerate(order):
+        r = T.rank_of(d)
+        off = T.reqland[:, 64 * r + 8 * me:64 * r + 8 * me + 8]
+        out = T.stage[:, CAP * k:CAP * k + CAP]
+        if k % 2 == 0:
+            need("v", "rq%d" % r, _n(hi) if d == peer else _n(lo))
+            ready.append(("v", v_(V.tensor_copy, out, win.indirect(off))))
+        else:
+            need("a", "rq%d" % r, _n(hi) if d == peer else _n(lo))
+            ready.append(("a", a_(out, win.indirect(off), Act.Copy)))
+    need("a", "v", v_rq)
+    a_own = a_(T.land[:, CAP * me:CAP * me + CAP], win.indirect(T.rq[:, 8 * me:8 * me + 8]), Act.Copy)
+
+    def blk(k):
+        return T.stage[:, CAP * k:CAP * k + CAP]
+
+    mine = T.land[:, CAP * me:CAP * me + CAP]
+    for i in (0, 1):
+        for k in (2 * i, 2 * i + 1):
+            need("gq", ready[k][0], ready[k][1])
+        g.remote_dma_fused([
+            RemoteDMATransfer(dst_ids=[did(relays[i])], dma_engine_mask=lo, remote_sem=T.sem.xd0, srcs=[blk(2 * i)],
+                              dsts=[T.xd[:, 0:CAP]], alu_op=0),
+            RemoteDMATransfer(dst_ids=[did(helper)], dma_engine_mask=hi, remote_sem=T.sem["xd%d" % i], srcs=[blk(2 * i + 1)],
+                              dsts=[T.xd[:, CAP * i:CAP * i + CAP]], alu_op=0),
+        ], local_sem=T.sem.snt)
+        sent += _n(lo) + _n(hi)
+    for k in (4, 5, 6):
+        need("gq", ready[k][0], ready[k][1])
+    g.remote_dma_fused([
+        RemoteDMATransfer(dst_ids=[did(X[0])], dma_engine_mask=lo_a, remote_sem=T.sem.arr, srcs=[blk(4)], dsts=[mine], alu_op=0),
+        RemoteDMATransfer(dst_ids=[did(X[1])], dma_engine_mask=lo_b, remote_sem=T.sem.arr, srcs=[blk(5)], dsts=[mine], alu_op=0),
+        RemoteDMATransfer(dst_ids=[did(peer)], dma_engine_mask=hi, remote_sem=T.sem.arr, srcs=[blk(6)], dsts=[mine], alu_op=0),
+    ], local_sem=T.sem.snt)
+    sent += _n(lo) + _n(hi)
+
+    total = _n(lo_a) + _n(lo_b) + _n(hi) + 4 * _n(lo)
+    lw = T.land[:, 0:NR * CAP]
+    need("a", "arr", total)
+    need("a", "v", v_fu)
+    a_odd = a_(T.tmpo[:, 0:128], lw.indirect(T.fu[:, 16:24]), Act.Copy)
+    need("v", "arr", total)
+    need("v", "a", a_own)
+    v_(V.tensor_copy, T.tmpo[:, 128:256], lw.indirect(T.fu[:, 24:32]))
+    need("v", "a", a_odd)
+    v_y = v_(V.tensor_tensor, T.ysb[:, :], lw.indirect(T.fu[:, 0:16]), T.tmpo[:, :], Op.add)
+    need("s", "v", v_y)
+    g.sync.dma_start(T.y[:, :], T.ysb[:, :]).then_inc(T.sem.st, 16)
+    g.sync.wait_ge(T.sem.st, 16)
+    g.wait_ge(T.sem.snt, sent)

@@ -3,7 +3,9 @@ from concourse.mybir import AluOpType, ActivationFunctionType
 
 Op, Act = AluOpType, ActivationFunctionType
 NR, COLS, CAP, BAGS = 8, 4096, 128, 256
-CA = 2560
+CA = COLS // 2
+NP = 4
+PW = 8 // NP
 
 SCRATCH = {
     "tabs": ("sbuf", [128, COLS], "float32"),
@@ -33,6 +35,7 @@ SCRATCH = {
     "rh": ("sbuf", [128, 256], "float32"),
     "rq": ("sbuf", [128, 64], "uint16"),
     "reqland": ("sbuf", [128, 512], "uint16"),
+    "fwl": ("sbuf", [128, 16], "uint16"),
     "stage": ("sbuf", [128, 7 * CAP], "float32"),
     "land": ("sbuf", [128, NR * CAP], "float32"),
     "xw": ("sbuf", [128, 144], "float32"),
@@ -42,13 +45,13 @@ SCRATCH = {
     "fu": ("sbuf", [128, 32], "uint16"),
     "tmpo": ("sbuf", [128, BAGS], "float32"),
     "ysb": ("sbuf", [128, BAGS], "float32"),
-    "xq": ("sbuf", [128, 64], "uint16"),
+    "xq": ("sbuf", [128, PW], "uint16"),
     "xd": ("sbuf", [128, 2 * CAP], "float32"),
     "cnt": ("psum", [128, 512], "float32"),
     "rqp": ("psum", [128, 512], "float32"),
     "fp": ("psum", [128, 512], "float32"),
 }
-SEMAPHORES = ["ld", "ta", "tb", "v", "p", "a", "gq", "s1", "snt", "arr", "xd0", "xd1", "st"] + ["rq%d" % q for q in range(NR)]
+SEMAPHORES = ["ld", "ta", "tb", "v", "p", "a", "gq", "pq", "fwq", "snt", "arr", "xd0", "xd1", "st"] + ["rq%d" % q for q in range(NR)]
 
 _CACHE = {}
 
@@ -62,7 +65,7 @@ def _plan(T, topo):
     def on_chip(c):
         return [x for x in world if topo.host(x) == topo.host(c) and topo.chip(x) == topo.chip(c)]
 
-    peer, S, X, D, helper, relay, role, pos = {}, {}, {}, {}, {}, {}, {}, {}
+    peer, S, X, D, helper, relay, role, pos, via = {}, {}, {}, {}, {}, {}, {}, {}, {}
     for s in ranks:
         mine = [x for x in ranks if x in on_chip(s)]
         pos[s] = mine.index(s)
@@ -72,15 +75,16 @@ def _plan(T, topo):
         X[s] = [x for x in ranks if x not in mine and x not in S[s] and x not in D[s]]
         role[s] = ("rank",)
     for s in ranks:
+        via[s] = X[s][pos[s]]
         free = [x for x in on_chip(s) if x not in ranks and topo.die(x) == topo.die(s)]
         helper[s] = free[pos[s]]
-        role[helper[s]] = ("helper", s)
+        role[helper[s]] = ("pass", s, S[s], s, 0)
         far = [x for x in on_chip(X[s][0]) if x not in ranks and topo.die(x) != topo.die(X[s][0])]
         for d in D[s]:
             r = far[2 * pos[s] + pos[d]]
             relay[(s, d)] = r
-            role[r] = ("relay", s, d)
-    _CACHE["plan"] = dict(peer=peer, S=S, X=X, D=D, helper=helper, relay=relay, role=role)
+            role[r] = ("pass", s, [d], via[s], 1 + pos[d])
+    _CACHE["plan"] = dict(peer=peer, S=S, X=X, D=D, helper=helper, relay=relay, role=role, via=via)
     return _CACHE["plan"]
 
 
@@ -92,23 +96,16 @@ def _n(m):
     return len(_bits(m))
 
 
-def _passer(g, core, T, topo, s, outs):
-    qs = T.rank_of(s)
+def _passer(g, core, T, topo, s, outs, a, j, b):
+    qs, qa, qb = T.rank_of(s), T.rank_of(a), T.rank_of(b)
     m = topo.mask(core, outs[0])
-    rsem = T.sem["rq%d" % qs]
+    npc = _n(topo.mask(a, core) & ~m) // NP
     nin = _n(topo.mask(s, core) & ~topo.mask(s, outs[0]))
-    g.wait_ge(rsem, nin)
-    ids = []
-    for d in outs:
-        rid, pid = topo.addr(d, core)
-        ids.append(DstId(rid=rid, pnc=pid))
-    if len(outs) == 1:
-        o = T.rank_of(outs[0])
-        src, dst = T.xq[:, 8 * o:8 * o + 8], T.reqland[:, 64 * qs + 8 * o:64 * qs + 8 * o + 8]
-    else:
-        src, dst = T.xq[:, :], T.reqland[:, 64 * qs:64 * qs + 64]
-    g.remote_dma_fused([RemoteDMATransfer(dst_ids=ids, dma_engine_mask=m, remote_sem=rsem, srcs=[src],
-                                          dsts=[dst for d in outs], alu_op=0)], local_sem=T.sem.snt)
+    g.wait_ge(T.sem.pq, npc)
+    rid, pid = topo.addr(b, core)
+    c0 = 64 * qa + 8 * qb + PW * j
+    g.remote_dma(out_ap=T.reqland[:, c0:c0 + PW], in_ap=T.xq[:, :], remote_sem=T.sem["rq%d" % qa], local_sem=T.sem.snt,
+                 pid=pid, routing_id=rid, dma_engine_mask=m)
     for i, d in enumerate(outs):
         rid, pid = topo.addr(d, core)
         g.wait_ge(T.sem["xd%d" % i], nin)
@@ -122,21 +119,21 @@ def rank_program(g, core, T, topo):
     role = plan["role"].get(core)
     if role is None:
         return
-    if role[0] == "helper":
-        _passer(g, core, T, topo, role[1], plan["S"][role[1]])
-        return
-    if role[0] == "relay":
-        _passer(g, core, T, topo, role[1], [role[2]])
+    if role[0] == "pass":
+        _passer(g, core, T, topo, role[1], role[2], role[3], role[4], plan["peer"][role[3]])
         return
 
     me = T.rank_of(core)
     peer, S, X, D = plan["peer"][core], plan["S"][core], plan["X"][core], plan["D"][core]
-    helper = plan["helper"][core]
+    helper, via = plan["helper"][core], plan["via"][core]
     relays = [plan["relay"][(core, d)] for d in D]
+    warm = [helper] + [plan["relay"][(via, d)] for d in plan["D"][via]]
     lo = topo.mask(core, X[0])
     hi = topo.mask(core, peer) & ~lo
-    lob = _bits(lo)
+    lob, hib = _bits(lo), _bits(hi)
     lo_a, lo_b = sum(lob[:len(lob) // 2]), sum(lob[len(lob) // 2:])
+    npc = len(hib) // NP
+    hip = [sum(hib[npc * j:npc * j + npc]) for j in range(NP)]
 
     def did(d):
         rid, pid = topo.addr(d, core)
@@ -175,7 +172,6 @@ def rank_program(g, core, T, topo):
 
     g.sync.dma_start(T.ei[:, :], T.idx[:, :]).then_inc(T.sem.ld, 16)
     g.sync.dma_start(T.tabs[:, 0:CA], T.tab[:, 0:CA]).then_inc(T.sem.ta, 16)
-    A.wait_ge(T.sem.s1, _n(lo) + _n(hi))
     A.dma_start(T.tabs[:, CA:COLS], T.tab[:, CA:COLS]).then_inc(T.sem.tb, 16)
 
     v_ones = v_(V.memset, T.ones[:, :], 1.0)
@@ -230,19 +226,36 @@ def rank_program(g, core, T, topo):
     v_rq = v_(V.tensor_copy, T.rq[:, :], T.rqp[:, 0:64])
 
     mysem = T.sem["rq%d" % me]
-    slot = T.reqland[:, 64 * me:64 * me + 64]
+
+    def lst(o):
+        return T.rq[:, 8 * T.rank_of(o):8 * T.rank_of(o) + 8]
+
+    def spot(q, o):
+        c = 64 * T.rank_of(q) + 8 * T.rank_of(o)
+        return T.reqland[:, c:c + 8]
+
+    def pair(two, srcs, dsts, sem):
+        g.remote_dma_fused([
+            RemoteDMATransfer(dst_ids=[did(two[i])], dma_engine_mask=(lo_a, lo_b)[i], remote_sem=sem, srcs=[srcs[i]],
+                              dsts=[dsts[i]], alu_op=0) for i in (0, 1)], local_sem=T.sem.snt)
+        return _n(lo)
+
     need("gq", "v", v_rq)
-    g.remote_dma_fused([
-        RemoteDMATransfer(dst_ids=[did(r) for r in relays], dma_engine_mask=lo, remote_sem=mysem, srcs=[T.rq[:, :]],
-                          dsts=[T.xq[:, :] for r in relays], alu_op=0),
-        RemoteDMATransfer(dst_ids=[did(helper), did(peer)], dma_engine_mask=hi, remote_sem=mysem, srcs=[T.rq[:, :]],
-                          dsts=[T.xq[:, :], slot], alu_op=0),
-    ], local_sem=T.sem.s1)
-    g.remote_dma_fused([
-        RemoteDMATransfer(dst_ids=[did(d) for d in X], dma_engine_mask=lo, remote_sem=mysem, srcs=[T.rq[:, :]],
-                          dsts=[slot for d in X], alu_op=0),
-    ], local_sem=T.sem.snt)
-    sent = _n(lo)
+    sent = pair([via, via], [lst(d) for d in D], [T.fwl[:, 0:8], T.fwl[:, 8:16]], T.sem.fwq)
+    sent += pair(S, [lst(d) for d in S], [spot(core, d) for d in S], mysem)
+    qp = 8 * T.rank_of(peer)
+    c0 = 64 * me + qp + PW * (NP - 1)
+    g.remote_dma_fused(
+        [RemoteDMATransfer(dst_ids=[did(w)], dma_engine_mask=hip[j], remote_sem=T.sem.pq, srcs=[T.rq[:, qp + PW * j:qp + PW * j + PW]],
+                           dsts=[T.xq[:, :]], alu_op=0) for j, w in enumerate(warm)] +
+        [RemoteDMATransfer(dst_ids=[did(peer)], dma_engine_mask=hip[NP - 1], remote_sem=mysem,
+                           srcs=[T.rq[:, qp + PW * (NP - 1):qp + 8]], dsts=[T.reqland[:, c0:c0 + PW]], alu_op=0)],
+        local_sem=T.sem.snt)
+    sent += _n(hi)
+    g.wait_ge(T.sem.fwq, _n(lo))
+    far = plan["D"][via]
+    sent += pair(far, [T.fwl[:, 0:8], T.fwl[:, 8:16]], [spot(via, d) for d in far], T.sem["rq%d" % T.rank_of(via)])
+    sent += pair(X, [lst(d) for d in X], [spot(core, d) for d in X], mysem)
 
     v_(V.tensor_scalar, T.ptmp[:, 0:1], T.pidx[:, :], 15, None, Op.bitwise_and)
     v_(V.tensor_scalar, T.ptmp[:, 1:2], T.pidx[:, :], 4, None, Op.logical_shift_right)
@@ -269,13 +282,14 @@ def rank_program(g, core, T, topo):
         need(q, "tb", 16)
     for k, d in enumerate(order):
         r = T.rank_of(d)
-        off = T.reqland[:, 64 * r + 8 * me:64 * r + 8 * me + 8]
+        off = spot(d, core)
         out = T.stage[:, CAP * k:CAP * k + CAP]
+        arrived = npc + (NP - 1) * _n(lo) if d == peer else _n(lo_a)
         if k % 2 == 0:
-            need("v", "rq%d" % r, _n(hi) if d == peer else _n(lo))
+            need("v", "rq%d" % r, arrived)
             ready.append(("v", v_(V.tensor_copy, out, win.indirect(off))))
         else:
-            need("a", "rq%d" % r, _n(hi) if d == peer else _n(lo))
+            need("a", "rq%d" % r, arrived)
             ready.append(("a", a_(out, win.indirect(off), Act.Copy)))
     need("a", "v", v_rq)
     a_own = a_(T.land[:, CAP * me:CAP * me + CAP], win.indirect(T.rq[:, 8 * me:8 * me + 8]), Act.Copy)
@@ -294,14 +308,13 @@ def rank_program(g, core, T, topo):
                               dsts=[T.xd[:, CAP * i:CAP * i + CAP]], alu_op=0),
         ], local_sem=T.sem.snt)
         sent += _n(lo) + _n(hi)
-    for k in (4, 5, 6):
+    for k in (4, 5):
         need("gq", ready[k][0], ready[k][1])
-    g.remote_dma_fused([
-        RemoteDMATransfer(dst_ids=[did(X[0])], dma_engine_mask=lo_a, remote_sem=T.sem.arr, srcs=[blk(4)], dsts=[mine], alu_op=0),
-        RemoteDMATransfer(dst_ids=[did(X[1])], dma_engine_mask=lo_b, remote_sem=T.sem.arr, srcs=[blk(5)], dsts=[mine], alu_op=0),
-        RemoteDMATransfer(dst_ids=[did(peer)], dma_engine_mask=hi, remote_sem=T.sem.arr, srcs=[blk(6)], dsts=[mine], alu_op=0),
-    ], local_sem=T.sem.snt)
-    sent += _n(lo) + _n(hi)
+    sent += pair(X, [blk(4), blk(5)], [mine, mine], T.sem.arr)
+    need("gq", ready[6][0], ready[6][1])
+    rid, pid = topo.addr(peer, core)
+    g.remote_dma(out_ap=mine, in_ap=blk(6), remote_sem=T.sem.arr, local_sem=T.sem.snt, pid=pid, routing_id=rid, dma_engine_mask=hi)
+    sent += _n(hi)
 
     total = _n(lo_a) + _n(lo_b) + _n(hi) + 4 * _n(lo)
     lw = T.land[:, 0:NR * CAP]

@@ -65,7 +65,7 @@ def _plan(T, topo):
     def on_chip(c):
         return [x for x in world if topo.host(x) == topo.host(c) and topo.chip(x) == topo.chip(c)]
 
-    peer, S, X, D, helper, relay, role, pos, via = {}, {}, {}, {}, {}, {}, {}, {}, {}
+    peer, S, X, D, relay, role, pos, via, xfw, xjob = {}, {}, {}, {}, {}, {}, {}, {}, {}, {}
     for s in ranks:
         mine = [x for x in ranks if x in on_chip(s)]
         pos[s] = mine.index(s)
@@ -76,15 +76,17 @@ def _plan(T, topo):
         role[s] = ("rank",)
     for s in ranks:
         via[s] = X[s][pos[s]]
-        free = [x for x in on_chip(s) if x not in ranks and topo.die(x) == topo.die(s)]
-        helper[s] = free[pos[s]]
-        role[helper[s]] = ("pass", s, S[s], s, 0)
         far = [x for x in on_chip(X[s][0]) if x not in ranks and topo.die(x) != topo.die(X[s][0])]
         for d in D[s]:
             r = far[2 * pos[s] + pos[d]]
             relay[(s, d)] = r
-            role[r] = ("pass", s, [d], via[s], 1 + pos[d])
-    _CACHE["plan"] = dict(peer=peer, S=S, X=X, D=D, helper=helper, relay=relay, role=role, via=via)
+            role[r] = ("pass", s, d, via[s], pos[d])
+        other = [x for x in on_chip(s) if x not in ranks and topo.die(x) != topo.die(s)]
+        for x in X[s]:
+            r = other[2 * pos[s] + 1 - pos[x]]
+            xfw[(s, x)] = r
+            xjob[r] = (s, x)
+    _CACHE["plan"] = dict(peer=peer, S=S, X=X, D=D, relay=relay, role=role, via=via, xfw=xfw, xjob=xjob)
     return _CACHE["plan"]
 
 
@@ -96,22 +98,29 @@ def _n(m):
     return len(_bits(m))
 
 
-def _passer(g, core, T, topo, s, outs, a, j, b):
-    qs, qa, qb = T.rank_of(s), T.rank_of(a), T.rank_of(b)
-    m = topo.mask(core, outs[0])
+def _passer(g, core, T, topo, s, d, a, j, b, xjob):
+    qa, qb = T.rank_of(a), T.rank_of(b)
+    xa, xx = xjob
+    m = topo.mask(core, d)
     npc = _n(topo.mask(a, core) & ~m) // NP
-    nin = _n(topo.mask(s, core) & ~topo.mask(s, outs[0]))
     g.wait_ge(T.sem.pq, npc)
     rid, pid = topo.addr(b, core)
-    c0 = 64 * qa + 8 * qb + PW * j
+    c0 = 64 * qa + 8 * qb + PW * (1 + j)
     g.remote_dma(out_ap=T.reqland[:, c0:c0 + PW], in_ap=T.xq[:, :], remote_sem=T.sem["rq%d" % qa], local_sem=T.sem.snt,
                  pid=pid, routing_id=rid, dma_engine_mask=m)
-    for i, d in enumerate(outs):
-        rid, pid = topo.addr(d, core)
+    left = _n(m)
+    jobs = [(s, d, 0, _n(topo.mask(s, core))), (xa, xx, 1, _n(topo.mask(xa, core) & ~topo.mask(xa, xx)))]
+    if j == 1:
+        jobs.reverse()
+    for own, dst, i, nin in jobs:
+        q = T.rank_of(own)
+        mo = topo.mask(core, dst)
+        rid, pid = topo.addr(dst, core)
         g.wait_ge(T.sem["xd%d" % i], nin)
-        g.remote_dma(out_ap=T.land[:, CAP * qs:CAP * qs + CAP], in_ap=T.xd[:, CAP * i:CAP * i + CAP], remote_sem=T.sem.arr,
-                     local_sem=T.sem.snt, pid=pid, routing_id=rid, dma_engine_mask=m)
-    g.wait_ge(T.sem.snt, _n(m) * (1 + len(outs)))
+        g.remote_dma(out_ap=T.land[:, CAP * q:CAP * q + CAP], in_ap=T.xd[:, CAP * i:CAP * i + CAP], remote_sem=T.sem.arr,
+                     local_sem=T.sem.snt, pid=pid, routing_id=rid, dma_engine_mask=mo)
+        left += _n(mo)
+    g.wait_ge(T.sem.snt, left)
 
 
 def rank_program(g, core, T, topo):
@@ -120,14 +129,15 @@ def rank_program(g, core, T, topo):
     if role is None:
         return
     if role[0] == "pass":
-        _passer(g, core, T, topo, role[1], role[2], role[3], role[4], plan["peer"][role[3]])
+        _passer(g, core, T, topo, role[1], role[2], role[3], role[4], plan["peer"][role[3]], plan["xjob"][core])
         return
 
     me = T.rank_of(core)
     peer, S, X, D = plan["peer"][core], plan["S"][core], plan["X"][core], plan["D"][core]
-    helper, via = plan["helper"][core], plan["via"][core]
+    via = plan["via"][core]
     relays = [plan["relay"][(core, d)] for d in D]
-    warm = [helper] + [plan["relay"][(via, d)] for d in plan["D"][via]]
+    xfs = [plan["xfw"][(core, x)] for x in X]
+    warm = [plan["relay"][(via, d)] for d in plan["D"][via]]
     lo = topo.mask(core, X[0])
     hi = topo.mask(core, peer) & ~lo
     lob, hib = _bits(lo), _bits(hi)
@@ -242,20 +252,21 @@ def rank_program(g, core, T, topo):
 
     need("gq", "v", v_rq)
     sent = pair([via, via], [lst(d) for d in D], [T.fwl[:, 0:8], T.fwl[:, 8:16]], T.sem.fwq)
-    sent += pair(S, [lst(d) for d in S], [spot(core, d) for d in S], mysem)
+    sent += pair(X, [lst(d) for d in X], [spot(core, d) for d in X], mysem)
     qp = 8 * T.rank_of(peer)
-    c0 = 64 * me + qp + PW * (NP - 1)
+    c0 = 64 * me + qp
     g.remote_dma_fused(
-        [RemoteDMATransfer(dst_ids=[did(w)], dma_engine_mask=hip[j], remote_sem=T.sem.pq, srcs=[T.rq[:, qp + PW * j:qp + PW * j + PW]],
-                           dsts=[T.xq[:, :]], alu_op=0) for j, w in enumerate(warm)] +
-        [RemoteDMATransfer(dst_ids=[did(peer)], dma_engine_mask=hip[NP - 1], remote_sem=mysem,
-                           srcs=[T.rq[:, qp + PW * (NP - 1):qp + 8]], dsts=[T.reqland[:, c0:c0 + PW]], alu_op=0)],
+        [RemoteDMATransfer(dst_ids=[did(warm[j - 1])], dma_engine_mask=hip[j], remote_sem=T.sem.pq,
+                           srcs=[T.rq[:, qp + PW * j:qp + PW * j + PW]], dsts=[T.xq[:, :]], alu_op=0) for j in (1, 2)] +
+        [RemoteDMATransfer(dst_ids=[did(peer)], dma_engine_mask=hip[j], remote_sem=mysem,
+                           srcs=[T.rq[:, qp + PW * j:qp + PW * j + PW]], dsts=[T.reqland[:, c0 + PW * j:c0 + PW * j + PW]],
+                           alu_op=0) for j in (0, NP - 1)],
         local_sem=T.sem.snt)
     sent += _n(hi)
     g.wait_ge(T.sem.fwq, _n(lo))
     far = plan["D"][via]
     sent += pair(far, [T.fwl[:, 0:8], T.fwl[:, 8:16]], [spot(via, d) for d in far], T.sem["rq%d" % T.rank_of(via)])
-    sent += pair(X, [lst(d) for d in X], [spot(core, d) for d in X], mysem)
+    sent += pair(S, [lst(d) for d in S], [spot(core, d) for d in S], mysem)
 
     v_(V.tensor_scalar, T.ptmp[:, 0:1], T.pidx[:, :], 15, None, Op.bitwise_and)
     v_(V.tensor_scalar, T.ptmp[:, 1:2], T.pidx[:, :], 4, None, Op.logical_shift_right)
@@ -274,7 +285,7 @@ def rank_program(g, core, T, topo):
     need("v", "p", p_f)
     v_fu = v_(V.tensor_copy, T.fu[:, :], T.fp[:, 0:32])
 
-    order = [D[0], S[0], D[1], S[1], X[0], X[1], peer]
+    order = [D[0], X[0], D[1], X[1], S[0], S[1], peer]
     win = T.tabs[:, 0:COLS]
     ready = []
     for q in ("v", "a"):
@@ -284,7 +295,7 @@ def rank_program(g, core, T, topo):
         r = T.rank_of(d)
         off = spot(d, core)
         out = T.stage[:, CAP * k:CAP * k + CAP]
-        arrived = npc + (NP - 1) * _n(lo) if d == peer else _n(lo_a)
+        arrived = 2 * npc + 2 * _n(lo) if d == peer else _n(lo_a)
         if k % 2 == 0:
             need("v", "rq%d" % r, arrived)
             ready.append(("v", v_(V.tensor_copy, out, win.indirect(off))))
@@ -304,19 +315,19 @@ def rank_program(g, core, T, topo):
         g.remote_dma_fused([
             RemoteDMATransfer(dst_ids=[did(relays[i])], dma_engine_mask=lo, remote_sem=T.sem.xd0, srcs=[blk(2 * i)],
                               dsts=[T.xd[:, 0:CAP]], alu_op=0),
-            RemoteDMATransfer(dst_ids=[did(helper)], dma_engine_mask=hi, remote_sem=T.sem["xd%d" % i], srcs=[blk(2 * i + 1)],
-                              dsts=[T.xd[:, CAP * i:CAP * i + CAP]], alu_op=0),
+            RemoteDMATransfer(dst_ids=[did(xfs[i])], dma_engine_mask=hi, remote_sem=T.sem.xd1, srcs=[blk(2 * i + 1)],
+                              dsts=[T.xd[:, CAP:2 * CAP]], alu_op=0),
         ], local_sem=T.sem.snt)
         sent += _n(lo) + _n(hi)
     for k in (4, 5):
         need("gq", ready[k][0], ready[k][1])
-    sent += pair(X, [blk(4), blk(5)], [mine, mine], T.sem.arr)
+    sent += pair(S, [blk(4), blk(5)], [mine, mine], T.sem.arr)
     need("gq", ready[6][0], ready[6][1])
     rid, pid = topo.addr(peer, core)
     g.remote_dma(out_ap=mine, in_ap=blk(6), remote_sem=T.sem.arr, local_sem=T.sem.snt, pid=pid, routing_id=rid, dma_engine_mask=hi)
     sent += _n(hi)
 
-    total = _n(lo_a) + _n(lo_b) + _n(hi) + 4 * _n(lo)
+    total = _n(hi) + _n(lo_a) + _n(lo_b) + 4 * _n(lo)
     lw = T.land[:, 0:NR * CAP]
     need("a", "arr", total)
     need("a", "v", v_fu)

from concourse.bass import DstId, RemoteDMATransfer
from concourse.mybir import AluOpType, ActivationFunctionType

Op, Act = AluOpType, ActivationFunctionType
NR, COLS, CAP, BAGS = 8, 4096, 128, 256
CA = COLS // 2
NP = 4
PW = 8 // NP

SCRATCH = {
    "tabs": ("sbuf", [128, COLS], "float32"),
    "ei": ("sbuf", [128, 4], "int32"),
    "owni": ("sbuf", [128, 4], "int32"),
    "loci": ("sbuf", [128, 4], "int32"),
    "locf": ("sbuf", [128, 4], "float32"),
    "pidx": ("sbuf", [128, 1], "int32"),
    "pbit": ("sbuf", [128, 1], "int32"),
    "ptmp": ("sbuf", [128, 2], "int32"),
    "pcol": ("sbuf", [128, 2], "float32"),
    "offa": ("sbuf", [128, 2], "uint16"),
    "iotar": ("sbuf", [128, 32], "int32"),
    "rst": ("sbuf", [128, 32], "float32"),
    "ohp": ("sbuf", [128, 56], "bfloat16"),
    "ones": ("sbuf", [128, 128], "bfloat16"),
    "tri": ("sbuf", [128, 128], "bfloat16"),
    "crow": ("sbuf", [128, 32], "bfloat16"),
    "prod": ("sbuf", [128, 32], "float32"),
    "seg": ("sbuf", [128, 32], "float32"),
    "ti": ("sbuf", [128, 4], "int32"),
    "hi": ("sbuf", [128, 4], "int32"),
    "hf": ("sbuf", [128, 4], "float32"),
    "im16": ("sbuf", [128, 128], "float32"),
    "i64": ("sbuf", [128, 64], "float32"),
    "lh": ("sbuf", [128, 512], "float32"),
    "rh": ("sbuf", [128, 256], "float32"),
    "rq": ("sbuf", [128, 64], "uint16"),
    "reqland": ("sbuf", [128, 512], "uint16"),
    "fwl": ("sbuf", [128, 16], "uint16"),
    "stage": ("sbuf", [128, 7 * CAP], "float32"),
    "land": ("sbuf", [128, NR * CAP], "float32"),
    "xw": ("sbuf", [128, 144], "float32"),
    "mw": ("sbuf", [128, 144], "float32"),
    "m16": ("sbuf", [128, 16], "float32"),
    "rfin": ("sbuf", [128, 64], "float32"),
    "fu": ("sbuf", [128, 32], "uint16"),
    "tmpo": ("sbuf", [128, BAGS], "float32"),
    "ysb": ("sbuf", [128, BAGS], "float32"),
    "xq": ("sbuf", [128, PW], "uint16"),
    "xd": ("sbuf", [128, 2 * CAP], "float32"),
    "cnt": ("psum", [128, 512], "float32"),
    "rqp": ("psum", [128, 512], "float32"),
    "fp": ("psum", [128, 512], "float32"),
}
SEMAPHORES = ["ld", "ta", "tb", "v", "p", "a", "gq", "pq", "fwq", "snt", "arr", "xd0", "xd1", "st"] + ["rq%d" % q for q in range(NR)]

_CACHE = {}


def _plan(T, topo):
    if "plan" in _CACHE:
        return _CACHE["plan"]
    ranks = list(T.cores)
    world = range(4 * topo.CORES_PER_HOST)

    def on_chip(c):
        return [x for x in world if topo.host(x) == topo.host(c) and topo.chip(x) == topo.chip(c)]

    peer, S, X, D, relay, role, pos, via, xfw, xjob = {}, {}, {}, {}, {}, {}, {}, {}, {}, {}
    for s in ranks:
        mine = [x for x in ranks if x in on_chip(s)]
        pos[s] = mine.index(s)
        peer[s] = [x for x in mine if x != s][0]
        S[s] = [x for x in ranks if topo.same_plane(s, x)]
        D[s] = [x for x in ranks if not topo.may_write(s, x)]
        X[s] = [x for x in ranks if x not in mine and x not in S[s] and x not in D[s]]
        role[s] = ("rank",)
    for s in ranks:
        via[s] = X[s][pos[s]]
        far = [x for x in on_chip(X[s][0]) if x not in ranks and topo.die(x) != topo.die(X[s][0])]
        for d in D[s]:
            r = far[2 * pos[s] + pos[d]]
            relay[(s, d)] = r
            role[r] = ("pass", s, d, via[s], pos[d])
        other = [x for x in on_chip(s) if x not in ranks and topo.die(x) != topo.die(s)]
        for x in X[s]:
            r = other[2 * pos[s] + 1 - pos[x]]
            xfw[(s, x)] = r
            xjob[r] = (s, x)
    _CACHE["plan"] = dict(peer=peer, S=S, X=X, D=D, relay=relay, role=role, via=via, xfw=xfw, xjob=xjob)
    return _CACHE["plan"]


def _bits(m):
    return [1 << i for i in range(m.bit_length()) if (m >> i) & 1]


def _n(m):
    return len(_bits(m))


def _passer(g, core, T, topo, s, d, a, j, b, xjob):
    qa, qb = T.rank_of(a), T.rank_of(b)
    xa, xx = xjob
    m = topo.mask(core, d)
    npc = _n(topo.mask(a, core) & ~m) // NP
    g.wait_ge(T.sem.pq, npc)
    rid, pid = topo.addr(b, core)
    c0 = 64 * qa + 8 * qb + PW * (1 + j)
    g.remote_dma(out_ap=T.reqland[:, c0:c0 + PW], in_ap=T.xq[:, :], remote_sem=T.sem["rq%d" % qa], local_sem=T.sem.snt,
                 pid=pid, routing_id=rid, dma_engine_mask=m)
    left = _n(m)
    jobs = [(s, d, 0, _n(topo.mask(s, core))), (xa, xx, 1, _n(topo.mask(xa, core) & ~topo.mask(xa, xx)))]
    if j == 1:
        jobs.reverse()
    for own, dst, i, nin in jobs:
        q = T.rank_of(own)
        mo = topo.mask(core, dst)
        rid, pid = topo.addr(dst, core)
        g.wait_ge(T.sem["xd%d" % i], nin)
        g.remote_dma(out_ap=T.land[:, CAP * q:CAP * q + CAP], in_ap=T.xd[:, CAP * i:CAP * i + CAP], remote_sem=T.sem.arr,
                     local_sem=T.sem.snt, pid=pid, routing_id=rid, dma_engine_mask=mo)
        left += _n(mo)
    g.wait_ge(T.sem.snt, left)


def rank_program(g, core, T, topo):
    plan = _plan(T, topo)
    role = plan["role"].get(core)
    if role is None:
        return
    if role[0] == "pass":
        _passer(g, core, T, topo, role[1], role[2], role[3], role[4], plan["peer"][role[3]], plan["xjob"][core])
        return

    me = T.rank_of(core)
    peer, S, X, D = plan["peer"][core], plan["S"][core], plan["X"][core], plan["D"][core]
    via = plan["via"][core]
    relays = [plan["relay"][(core, d)] for d in D]
    xfs = [plan["xfw"][(core, x)] for x in X]
    warm = [plan["relay"][(via, d)] for d in plan["D"][via]]
    lo = topo.mask(core, X[0])
    hi = topo.mask(core, peer) & ~lo
    lob, hib = _bits(lo), _bits(hi)
    lo_a, lo_b = sum(lob[:len(lob) // 2]), sum(lob[len(lob) // 2:])
    npc = len(hib) // NP
    hip = [sum(hib[npc * j:npc * j + npc]) for j in range(NP)]

    def did(d):
        rid, pid = topo.addr(d, core)
        return DstId(rid=rid, pnc=pid)

    Q = {"v": g.vector, "p": g.tensor, "a": g.scalar, "gq": g, "s": g.sync}
    cnt = {"v": 0, "p": 0, "a": 0, "gq": 0}
    seen = {}

    def need(q, sem, val):
        if val > seen.get((q, sem), 0):
            Q[q].wait_ge(T.sem[sem], val)
            seen[(q, sem)] = val

    def pre(q):
        need(q, q, cnt[q])

    def done(q, ins):
        ins.then_inc(T.sem[q], 1)
        cnt[q] += 1
        return cnt[q]

    V, PE, A = g.vector, g.tensor, g.scalar

    def v_(fn, *a, **k):
        pre("v")
        return done("v", fn(*a, **k))

    def g_(fn, *a, **k):
        pre("gq")
        return done("gq", fn(*a, **k))

    def a_(*a, **k):
        pre("a")
        return done("a", A.activation(*a, **k))

    g.sync.dma_start(T.ei[:, :], T.idx[:, :]).then_inc(T.sem.ld, 16)
    g.sync.dma_start(T.tabs[:, 0:CA], T.tab[:, 0:CA]).then_inc(T.sem.ta, 16)
    A.dma_start(T.tabs[:, CA:COLS], T.tab[:, CA:COLS]).then_inc(T.sem.tb, 16)

    v_ones = v_(V.memset, T.ones[:, :], 1.0)
    v_(V.memset, T.ohp[:, 0:24], 0.0)
    g_pidx = g_(g.iota, T.pidx[:, :], [[0, 1]], 0, 1)
    g_iotar = g_(g.iota, T.iotar[:, :], [[0, 4], [1, 8]], 0, 0)
    g_crow = g_(g.iota, T.crow[0:1, :], [[0, 4], [CAP, 8]], 0, 0, allow_small_or_imprecise_dtypes=True)
    need("gq", "v", v_ones)
    g_tri = g_(g.affine_select, T.tri[:, :], T.ones[:, :], [[1, 128]], Op.is_gt, 0.0, 0, -1)
    g_im16 = g_(g.iota, T.im16[:, :], [[0, 8], [1, 16]], 0, 0, allow_small_or_imprecise_dtypes=True)
    g_i64 = g_(g.iota, T.i64[:, :], [[16, 64]], 0, 0, allow_small_or_imprecise_dtypes=True)
    g_xw = g_(g.iota, T.xw[:, :], [[0, 9], [-100, 2], [1, 8]], 100, 0, allow_small_or_imprecise_dtypes=True)

    need("v", "gq", g_pidx)
    v_(V.tensor_scalar, T.pbit[:, :], T.pidx[:, :], 3, 1, Op.logical_shift_right, Op.bitwise_and)
    v_(V.tensor_scalar, T.offa[:, 0:1], T.pbit[:, :], 0, None, Op.add)
    v_(V.tensor_scalar, T.offa[:, 1:2], T.pbit[:, :], 2, None, Op.add)
    need("v", "gq", g_iotar)
    v_(V.tensor_scalar, T.rst[:, :], T.iotar[:, :], 0, None, Op.not_equal)

    need("p", "gq", g_crow)
    need("p", "v", v_ones)
    PE.matmul(T.cnt[:, 0:32], T.ones[0:1, :], T.crow[0:1, :], True, False)

    need("v", "ld", 16)
    v_(V.tensor_scalar, T.owni[:, :], T.ei[:, :], 12, None, Op.logical_shift_right)
    v_oh = v_(V.tensor_tensor, T.ohp[:, 24:56], T.owni[:, 0:4].indirect(T.offa[:, 0:2]), T.iotar[:, :], Op.is_equal)
    need("p", "v", v_oh)
    need("p", "gq", g_tri)
    PE.matmul(T.cnt[:, 0:32], T.tri[:, :], T.ohp[:, 24:56], False, False)
    for k in (1, 2, 3):
        ins = PE.matmul(T.cnt[:, 0:32], T.ones[:, :], T.ohp[:, 24 - 8 * k:56 - 8 * k], False, k == 3)
    p_cnt = done("p", ins)
    v_(V.tensor_scalar, T.loci[:, :], T.ei[:, :], COLS - 1, None, Op.bitwise_and)
    v_(V.tensor_copy, T.locf[:, :], T.loci[:, :])
    need("v", "p", p_cnt)
    v_(V.tensor_tensor, T.prod[:, :], T.ohp[:, 24:56], T.cnt[:, 0:32], Op.mult)
    v_(V.tensor_tensor_scan, T.seg[:, :], T.rst[:, :], T.prod[:, :], 0.0, Op.mult, Op.add)
    v_(V.tensor_copy, T.ti[:, :], T.seg[:, 7:32:8])
    v_(V.tensor_scalar, T.hi[:, :], T.ti[:, :], NR * CAP - 16, None, Op.bitwise_and)
    v_(V.tensor_copy, T.hf[:, :], T.hi[:, :])

    need("v", "gq", g_i64)
    for C in range(4):
        t_c, h_c = T.seg[:, 8 * C + 7:8 * C + 8], T.hf[:, C:C + 1]
        v_(V.tensor_scalar, T.rh[:, 64 * C:64 * C + 64], T.i64[:, :], h_c, T.locf[:, C:C + 1], Op.is_equal, Op.mult)
        k = v_(V.tensor_scalar, T.lh[:, 128 * C:128 * C + 128], T.im16[:, :], h_c, t_c, Op.add, Op.is_equal)
        need("p", "v", k)
        ins = PE.matmul(T.rqp[:, 0:64], T.lh[:, 128 * C:128 * C + 128], T.rh[:, 64 * C:64 * C + 64], C == 0, C == 3)
    p_rq = done("p", ins)
    need("v", "p", p_rq)
    v_rq = v_(V.tensor_copy, T.rq[:, :], T.rqp[:, 0:64])

    mysem = T.sem["rq%d" % me]

    def lst(o):
        return T.rq[:, 8 * T.rank_of(o):8 * T.rank_of(o) + 8]

    def spot(q, o):
        c = 64 * T.rank_of(q) + 8 * T.rank_of(o)
        return T.reqland[:, c:c + 8]

    def pair(two, srcs, dsts, sem):
        g.remote_dma_fused([
            RemoteDMATransfer(dst_ids=[did(two[i])], dma_engine_mask=(lo_a, lo_b)[i], remote_sem=sem, srcs=[srcs[i]],
                              dsts=[dsts[i]], alu_op=0) for i in (0, 1)], local_sem=T.sem.snt)
        return _n(lo)

    need("gq", "v", v_rq)
    sent = pair([via, via], [lst(d) for d in D], [T.fwl[:, 0:8], T.fwl[:, 8:16]], T.sem.fwq)
    sent += pair(X, [lst(d) for d in X], [spot(core, d) for d in X], mysem)
    qp = 8 * T.rank_of(peer)
    c0 = 64 * me + qp
    g.remote_dma_fused(
        [RemoteDMATransfer(dst_ids=[did(warm[j - 1])], dma_engine_mask=hip[j], remote_sem=T.sem.pq,
                           srcs=[T.rq[:, qp + PW * j:qp + PW * j + PW]], dsts=[T.xq[:, :]], alu_op=0) for j in (1, 2)] +
        [RemoteDMATransfer(dst_ids=[did(peer)], dma_engine_mask=hip[j], remote_sem=mysem,
                           srcs=[T.rq[:, qp + PW * j:qp + PW * j + PW]], dsts=[T.reqland[:, c0 + PW * j:c0 + PW * j + PW]],
                           alu_op=0) for j in (0, NP - 1)],
        local_sem=T.sem.snt)
    sent += _n(hi)
    g.wait_ge(T.sem.fwq, _n(lo))
    far = plan["D"][via]
    sent += pair(far, [T.fwl[:, 0:8], T.fwl[:, 8:16]], [spot(via, d) for d in far], T.sem["rq%d" % T.rank_of(via)])
    sent += pair(S, [lst(d) for d in S], [spot(core, d) for d in S], mysem)

    v_(V.tensor_scalar, T.ptmp[:, 0:1], T.pidx[:, :], 15, None, Op.bitwise_and)
    v_(V.tensor_scalar, T.ptmp[:, 1:2], T.pidx[:, :], 4, None, Op.logical_shift_right)
    v_(V.tensor_copy, T.pcol[:, :], T.ptmp[:, :])
    v_(V.tensor_scalar, T.m16[:, :], T.im16[:, 0:16], T.pcol[:, 0:1], None, Op.is_equal)
    need("v", "gq", g_xw)
    v_(V.tensor_scalar, T.mw[:, :], T.xw[:, :], T.pcol[:, 1:2], None, Op.is_equal)
    for eta in (0, 1):
        for nu in (0, 1):
            C = 2 * nu + eta
            k = v_(V.tensor_scalar, T.rfin[:, 32 * eta + nu:32 * eta + 32:2], T.m16[:, :], T.seg[:, 8 * C + 7:8 * C + 8], None,
                   Op.mult)
    need("p", "v", k)
    PE.matmul(T.fp[:, 0:32], T.mw[:, 8:136], T.rfin[:, 0:32], True, False)
    p_f = done("p", PE.matmul(T.fp[:, 0:32], T.mw[:, 0:128], T.rfin[:, 32:64], False, True))
    need("v", "p", p_f)
    v_fu = v_(V.tensor_copy, T.fu[:, :], T.fp[:, 0:32])

    order = [D[0], X[0], D[1], X[1], S[0], S[1], peer]
    win = T.tabs[:, 0:COLS]
    ready = []
    for q in ("v", "a"):
        need(q, "ta", 16)
        need(q, "tb", 16)
    for k, d in enumerate(order):
        r = T.rank_of(d)
        off = spot(d, core)
        out = T.stage[:, CAP * k:CAP * k + CAP]
        arrived = 2 * npc + 2 * _n(lo) if d == peer else _n(lo_a)
        if k % 2 == 0:
            need("v", "rq%d" % r, arrived)
            ready.append(("v", v_(V.tensor_copy, out, win.indirect(off))))
        else:
            need("a", "rq%d" % r, arrived)
            ready.append(("a", a_(out, win.indirect(off), Act.Copy)))
    need("a", "v", v_rq)
    a_own = a_(T.land[:, CAP * me:CAP * me + CAP], win.indirect(T.rq[:, 8 * me:8 * me + 8]), Act.Copy)

    def blk(k):
        return T.stage[:, CAP * k:CAP * k + CAP]

    mine = T.land[:, CAP * me:CAP * me + CAP]
    for i in (0, 1):
        for k in (2 * i, 2 * i + 1):
            need("gq", ready[k][0], ready[k][1])
        g.remote_dma_fused([
            RemoteDMATransfer(dst_ids=[did(relays[i])], dma_engine_mask=lo, remote_sem=T.sem.xd0, srcs=[blk(2 * i)],
                              dsts=[T.xd[:, 0:CAP]], alu_op=0),
            RemoteDMATransfer(dst_ids=[did(xfs[i])], dma_engine_mask=hi, remote_sem=T.sem.xd1, srcs=[blk(2 * i + 1)],
                              dsts=[T.xd[:, CAP:2 * CAP]], alu_op=0),
        ], local_sem=T.sem.snt)
        sent += _n(lo) + _n(hi)
    for k in (4, 5):
        need("gq", ready[k][0], ready[k][1])
    sent += pair(S, [blk(4), blk(5)], [mine, mine], T.sem.arr)
    need("gq", ready[6][0], ready[6][1])
    rid, pid = topo.addr(peer, core)
    g.remote_dma(out_ap=mine, in_ap=blk(6), remote_sem=T.sem.arr, local_sem=T.sem.snt, pid=pid, routing_id=rid, dma_engine_mask=hi)
    sent += _n(hi)

    total = _n(hi) + _n(lo_a) + _n(lo_b) + 4 * _n(lo)
    lw = T.land[:, 0:NR * CAP]
    need("a", "arr", total)
    need("a", "v", v_fu)
    a_odd = a_(T.tmpo[:, 0:128], lw.indirect(T.fu[:, 16:24]), Act.Copy)
    need("v", "arr", total)
    need("v", "a", a_own)
    v_(V.tensor_copy, T.tmpo[:, 128:256], lw.indirect(T.fu[:, 24:32]))
    need("v", "a", a_odd)
    v_y = v_(V.tensor_tensor, T.ysb[:, :], lw.indirect(T.fu[:, 0:16]), T.tmpo[:, :], Op.add)
    need("s", "v", v_y)
    g.sync.dma_start(T.y[:, :], T.ysb[:, :]).then_inc(T.sem.st, 16)
    g.sync.wait_ge(T.sem.st, 16)
    g.wait_ge(T.sem.snt, sent)
